import numpy as np
import ml_dtypes


def mxq(x, axis, fmt="e4m3"):
    dtype, down = {"e4m3": (ml_dtypes.float8_e4m3fn, 7), "e5m2": (ml_dtypes.float8_e5m2, 14)}[fmt]
    v = np.moveaxis(np.asarray(x, np.float32).astype(ml_dtypes.bfloat16).astype(np.float64), axis, -1)
    blocks = v.reshape(v.shape[:-1] + (-1, 32))
    amax = np.abs(blocks).max(-1, keepdims=True)
    byte = np.maximum(np.where(amax > 0, np.frexp(amax)[1] - 1 + 127, 0) - down, 1)
    scale = np.exp2(byte - 127.0)
    codes = (blocks / scale).astype(np.float32).astype(dtype).astype(np.float64)
    return np.moveaxis((codes * scale).reshape(v.shape), -1, axis)


WIDE = False


def mx_kscale(k):
    if not WIDE:
        return np.ones(k)
    levels = np.array([10, -10, 5, -5, 0])
    if k % 512:
        return np.exp2(np.random.permutation(np.resize(levels, k // 32))).repeat(32)
    a = np.empty((k // 512, 16))
    for p in range(k // 512):
        a[p, :8] = np.random.permutation(np.resize(levels, 8))
        for g in range(8):
            far = levels[np.abs(levels - a[p, g]) >= 10]
            a[p, g + 8] = far[np.random.randint(len(far))]
    return np.exp2(a.ravel()).repeat(32)


def f64(x):
    return np.asarray(x).astype(np.float64)


def striped(idx):
    return np.tile(np.asarray(idx).reshape(-1, 16).T, (8, 1)).astype(np.uint16)


def unstriped(offs):
    return offs[:16].T.reshape(-1).astype(np.int64)


G, K, T, D, M = 512, 4, 2048, 512, 512


def setup_inputs():
    n = np.random.standard_normal
    s = mx_kscale(D)[:, None]
    grid = lambda x: np.round(x * 32) / 32
    x = grid(n((D, T))) * s
    idx = np.random.randint(0, T, (G, K))
    part = np.random.randint(1, 128 // K, (G, K)) / 64.0
    return {
        "xT": x.astype(np.float32),
        "w": (n((D, M)) / np.sqrt(D) / s).astype(np.float32),
        "part": np.tile(part.reshape(-1), (128, 1)).astype(np.float32),
        "bias": (0.3 * n((M, 1))).astype(np.float32),
        "offs": striped(idx.reshape(-1)),
    }


def reference(xT, w, part, bias, offs):
    x = f64(xT)[:, unstriped(offs)]
    y = mxq(f64(w), 0, "e4m3").T @ mxq((x * f64(part)[:1]).reshape(D, G, K).sum(-1), 0, "e4m3")
    y = y + f64(bias)
    y = np.maximum(y, 0.0)
    return y

@@ -1,0 +1,207 @@
+from contextlib import ExitStack
+
+import concourse.mybir as mybir
+from concourse.masks import make_identity
+
+G, J, T, D, M = 512, 4, 2048, 512, 512
+P = 128
+FLOPS = 2 * D * M * G
+BYTES = 4 * (D * T + D * M + G * J + M + M * G) + 2 * P * G * J // 16
+
+F32 = mybir.dt.float32
+BF16 = mybir.dt.bfloat16
+U32 = mybir.dt.uint32
+U16 = mybir.dt.uint16
+U8 = mybir.dt.uint8
+FP8X4 = mybir.dt.float8_e4m3fn_x4
+ADD, MULT, MAX = mybir.AluOpType.add, mybir.AluOpType.mult, mybir.AluOpType.max
+COPY, RELU = mybir.ActivationFunctionType.Copy, mybir.ActivationFunctionType.Relu
+
+Q = G // P
+C = P * J
+MT = M // P
+XC = 512
+V_COLS = 344
+
+
+def tile_attend_grid_relu_kernel(tc, xT, w, part, bias, offs, out):
+    nc = tc.nc
+    with ExitStack() as ctx:
+        keep = ctx.enter_context(tc.tile_pool(name="keep", bufs=1))
+        ring = ctx.enter_context(tc.tile_pool(name="ring", bufs=2))
+        psum = ctx.enter_context(tc.psum_pool(name="psum", bufs=2))
+        psum1 = ctx.enter_context(tc.psum_pool(name="psum1", bufs=1))
+
+        offsets = keep.tile([P, G * J // 16], U16, name="offsets")
+        nc.sync.dma_start(offsets[:], offs)
+
+        x_rows = xT.rearrange("(p h u) c -> p h u c", h=2, u=2)
+        raw = [[keep.tile([P, 2, XC], F32, name=f"raw{h}_{i}") for i in range(T // XC)] for h in range(2)]
+        for h in range(2):
+            for i in range(T // XC):
+                nc.sync.dma_start(out=raw[h][i][:], in_=x_rows[:, h, :, i * XC : (i + 1) * XC])
+        w_raw = keep.tile([P, 4, M], F32, name="w_raw")
+        nc.sync.dma_start(out=w_raw[:], in_=w.rearrange("(p t) m -> p t m", t=4))
+
+        rows = keep.tile([P, C], F32, name="rows")
+        brow = keep.tile([P, P], F32, name="brow")
+        nc.vector.memset(rows[:], 0.0)
+        nc.vector.memset(brow[:], 0.0)
+        nc.scalar.dma_start(out=rows[0:Q, :], in_=part[0:1, :].rearrange("o (q c) -> (o q) c", q=Q))
+        nc.scalar.dma_start(out=brow[0:MT, :], in_=bias.rearrange("(t p) o -> t (p o)", p=P))
+        ident_f = keep.tile([P, P], F32, name="ident_f")
+        make_identity(nc, ident_f[:])
+        ident_b = keep.tile([P, P], BF16, name="ident_b")
+        make_identity(nc, ident_b[:])
+
+        pt = psum.tile([P, J, P], F32, name="pt", tag="ts")
+        for j in range(J):
+            nc.tensor.transpose(pt[:, j, :], rows[:].rearrange("p (g j) -> p j g", j=J)[:, j, :], ident_f[:])
+        bt = psum.tile([P, P], F32, name="bt", tag="tv")
+        nc.tensor.transpose(bt[:], brow[:], ident_f[:])
+        part_t = keep.tile([P, J, Q], F32, name="part_t")
+        nc.vector.tensor_copy(out=part_t[:], in_=pt[:, :, 0:Q])
+        bias_t = keep.tile([P, MT], F32, name="bias_t")
+        nc.vector.tensor_copy(out=bias_t[:], in_=bt[:, 0:MT])
+
+        win = [keep.tile([P, 2 * T], BF16, name=f"win{h}") for h in range(2)]
+
+        def cast(engine_copy, h, i, lo, hi):
+            dst = win[h][:, 2 * (i * XC + lo) : 2 * (i * XC + hi)].rearrange("p (c u) -> p c u", u=2)
+            engine_copy(out=dst, in_=raw[h][i][:, :, lo:hi].rearrange("p u c -> p c u"))
+
+        def scalar_cast(out, in_):
+            nc.scalar.activation(out, in_, COPY)
+
+        cast(nc.vector.tensor_copy, 0, 0, 0, XC)
+        cast(scalar_cast, 0, 1, 0, XC)
+        cast(nc.vector.tensor_copy, 0, 2, 0, XC)
+        cast(nc.vector.tensor_copy, 0, 3, 0, V_COLS)
+        cast(scalar_cast, 0, 3, V_COLS, XC)
+        for i in range(T // XC):
+            cast(scalar_cast, 1, i, 0, XC)
+
+        w_group = keep.tile([P, M, 4], BF16, name="w_group", align_bytes=64)
+        nc.gpsimd.tensor_scalar(
+            out=w_group[:], in0=w_raw[:].rearrange("p t m -> p m t"), scalar1=1.0, scalar2=0.0, op0=MULT, op1=ADD
+        )
+        w_codes = keep.tile([P, M], U32, name="w_codes", align_bytes=64)
+        w_scales = keep.tile([P, M], U8, name="w_scales", align_bytes=64)
+
+        got = [[keep.tile([P, C], U32, name=f"got{h}_{q}") for q in range(Q)] for h in range(2)]
+
+        def gather(h, q):
+            nc.vector.tensor_copy(
+                got[h][q][:], win[h][:].bitcast(U32).indirect(offsets[:, q * C // 16 : (q + 1) * C // 16])
+            )
+
+        banks, terms, esum, turned, codes = {}, {}, {}, {}, {}
+
+        def forward(q):
+            ts = psum.tile([P, 2, 4, P], BF16, name="ts", tag="ts")
+            tv = psum.tile([P, 2, 4, P], BF16, name="tv", tag="tv")
+            banks[q] = (ts, tv)
+            for h in range(2):
+                src = got[h][q][:].bitcast(BF16).rearrange("p (g j u) -> p j u g", j=J, u=2)
+                for j in range(J):
+                    for u in range(2):
+                        nc.tensor.transpose((ts, tv)[j // 2][:, j % 2, 2 * h + u, :], src[:, j, u, :], ident_b[:])
+
+        def products(q):
+            p0 = ring.tile([P, 4, P], F32, name="p0")
+            p1 = ring.tile([P, 4, P], F32, name="p1")
+            terms[q] = (p0, p1)
+            for j, dst in ((0, p0), (1, p1)):
+                nc.scalar.activation(dst[:], banks[q][0][:, j, :, :], COPY, scale=part_t[:, j, q : q + 1])
+
+        def sums(q):
+            a = ring.tile([P, 4, P], F32, name="a")
+            b = ring.tile([P, 4, P], F32, name="b")
+            e = ring.tile([P, 4, P], BF16, name="e")
+            for j, src, dst in ((2, terms[q][0], a), (3, terms[q][1], b)):
+                nc.vector.scalar_tensor_tensor(
+                    out=dst[:], in0=banks[q][1][:, j - 2, :, :], scalar=part_t[:, j, q : q + 1], in1=src[:], op0=MULT, op1=ADD
+                )
+            adder = nc.vector if q == Q - 1 else nc.gpsimd
+            adder.tensor_tensor(out=e[:], in0=a[:], in1=b[:], op=ADD)
+            esum[q] = e
+
+        def back(q):
+            tb = psum1.tile([P, 4, P], BF16, name="tb")
+            for t in range(4):
+                nc.tensor.transpose(tb[:, t, :], esum[q][:, t, :], ident_b[:])
+            grouped = ring.tile([P, P, 4], BF16, name="grouped", align_bytes=64)
+            nc.scalar.copy(out=grouped[:], in_=tb[:].rearrange("p t g -> p g t"))
+            turned[q] = grouped
+
+        def quantise(q):
+            ec = ring.tile([P, P], U32, name="ec", align_bytes=64)
+            es = ring.tile([P, P], U8, name="es", align_bytes=64)
+            nc.vector.quantize_mx(
+                out=ec[:].bitcast(FP8X4), scales=es[:], in_=turned[q][:].rearrange("p g t -> p (g t)")
+            )
+            codes[q] = (ec, es)
+
+        out_rows = out.rearrange("(t p) g -> p t g", p=P)
+
+        def layer(q):
+            ec, es = codes[q]
+            o = ring.tile([P, MT, P], F32, name="o")
+            for half in range(2):
+                y = psum1.tile([P, 2, P], F32, name=f"y{half}")
+                for i in range(2):
+                    cols = slice((2 * half + i) * P, (2 * half + i + 1) * P)
+                    nc.tensor.matmul_mx(
+                        out=y[:, i, :],
+                        lhsT=w_codes[:, cols].bitcast(FP8X4),
+                        lhsT_scale=w_scales[:, cols],
+                        rhs=ec[:].bitcast(FP8X4),
+                        rhs_scale=es[:],
+                        start=True,
+                        stop=True,
+                    )
+                for i in range(2):
+                    mt = 2 * half + i
+                    if q == Q - 1 and half == 1:
+                        nc.vector.tensor_scalar(
+                            out=o[:, mt, :], in0=y[:, i, :], scalar1=bias_t[:, mt : mt + 1], scalar2=0.0, op0=ADD, op1=MAX
+                        )
+                    else:
+                        nc.scalar.activation(o[:, mt, :], y[:, i, :], RELU, bias=bias_t[:, mt : mt + 1])
+                nc.sync.dma_start(
+                    out=out_rows[:, 2 * half : 2 * half + 2, q * P : (q + 1) * P], in_=o[:, 2 * half : 2 * half + 2, :]
+                )
+
+        for q in range(Q):
+            gather(0, q)
+        gather(1, 0)
+        forward(0)
+        products(0)
+        gather(1, 1)
+        forward(1)
+        products(1)
+        sums(0)
+        gather(1, 2)
+        gather(1, 3)
+        back(0)
+        forward(2)
+        products(2)
+        sums(1)
+        nc.vector.quantize_mx(
+            out=w_codes[:].bitcast(FP8X4), scales=w_scales[:], in_=w_group[:].rearrange("p m t -> p (m t)")
+        )
+        quantise(0)
+        layer(0)
+        back(1)
+        forward(3)
+        products(3)
+        sums(2)
+        quantise(1)
+        layer(1)
+        back(2)
+        sums(3)
+        quantise(2)
+        layer(2)
+        back(3)
+        quantise(3)
+        layer(3)

@@ -21,7 +21,6 @@ Q = G // P
 C = P * J
 MT = M // P
 XC = 512
-V_COLS = 344
 
 
 def tile_attend_grid_relu_kernel(tc, xT, w, part, bias, offs, out):
@@ -29,64 +28,66 @@ def tile_attend_grid_relu_kernel(tc, xT, w, part, bias, offs, out):
     with ExitStack() as ctx:
         keep = ctx.enter_context(tc.tile_pool(name="keep", bufs=1))
         ring = ctx.enter_context(tc.tile_pool(name="ring", bufs=2))
+        ring3 = ctx.enter_context(tc.tile_pool(name="ring3", bufs=3))
+        psum4 = ctx.enter_context(tc.psum_pool(name="psum4", bufs=4))
         psum = ctx.enter_context(tc.psum_pool(name="psum", bufs=2))
         psum1 = ctx.enter_context(tc.psum_pool(name="psum1", bufs=1))
 
+        rows = keep.tile([P, C], F32, name="rows")
+        nc.gpsimd.memset(rows[:], 0.0)
         offsets = keep.tile([P, G * J // 16], U16, name="offsets")
         nc.sync.dma_start(offsets[:], offs)
-
         x_rows = xT.rearrange("(p h u) c -> p h u c", h=2, u=2)
         raw = [[keep.tile([P, 2, XC], F32, name=f"raw{h}_{i}") for i in range(T // XC)] for h in range(2)]
         for h in range(2):
             for i in range(T // XC):
                 nc.sync.dma_start(out=raw[h][i][:], in_=x_rows[:, h, :, i * XC : (i + 1) * XC])
+                if h == 0 and i == 1:
+                    nc.sync.dma_start(out=rows[0:Q, :], in_=part[0:1, :].rearrange("o (q c) -> (o q) c", q=Q))
         w_raw = keep.tile([P, 4, M], F32, name="w_raw")
         nc.sync.dma_start(out=w_raw[:], in_=w.rearrange("(p t) m -> p t m", t=4))
+        bias_t = keep.tile([P, MT], F32, name="bias_t")
+        nc.sync.dma_start(out=bias_t[:], in_=bias.rearrange("(t p) o -> p (t o)", p=P))
 
-        rows = keep.tile([P, C], F32, name="rows")
-        brow = keep.tile([P, P], F32, name="brow")
-        nc.vector.memset(rows[:], 0.0)
-        nc.vector.memset(brow[:], 0.0)
-        nc.scalar.dma_start(out=rows[0:Q, :], in_=part[0:1, :].rearrange("o (q c) -> (o q) c", q=Q))
-        nc.scalar.dma_start(out=brow[0:MT, :], in_=bias.rearrange("(t p) o -> t (p o)", p=P))
         ident_f = keep.tile([P, P], F32, name="ident_f")
         make_identity(nc, ident_f[:])
         ident_b = keep.tile([P, P], BF16, name="ident_b")
         make_identity(nc, ident_b[:])
 
-        pt = psum.tile([P, J, P], F32, name="pt", tag="ts")
-        for j in range(J):
-            nc.tensor.transpose(pt[:, j, :], rows[:].rearrange("p (g j) -> p j g", j=J)[:, j, :], ident_f[:])
-        bt = psum.tile([P, P], F32, name="bt", tag="tv")
-        nc.tensor.transpose(bt[:], brow[:], ident_f[:])
         part_t = keep.tile([P, J, Q], F32, name="part_t")
-        nc.vector.tensor_copy(out=part_t[:], in_=pt[:, :, 0:Q])
-        bias_t = keep.tile([P, MT], F32, name="bias_t")
-        nc.vector.tensor_copy(out=bias_t[:], in_=bt[:, 0:MT])
+
+        def parts():
+            pt = psum.tile([P, J, P], F32, name="pt", tag="acc")
+            for j in range(J):
+                nc.tensor.transpose(pt[:, j, :], rows[:].rearrange("p (g j) -> p j g", j=J)[:, j, :], ident_f[:])
+            nc.vector.tensor_copy(out=part_t[:], in_=pt[:, :, 0:Q])
 
         win = [keep.tile([P, 2 * T], BF16, name=f"win{h}") for h in range(2)]
 
-        def cast(engine_copy, h, i, lo, hi):
+        def cast(h, i, on_vector, lo=0, hi=XC):
             dst = win[h][:, 2 * (i * XC + lo) : 2 * (i * XC + hi)].rearrange("p (c u) -> p c u", u=2)
-            engine_copy(out=dst, in_=raw[h][i][:, :, lo:hi].rearrange("p u c -> p c u"))
-
-        def scalar_cast(out, in_):
-            nc.scalar.activation(out, in_, COPY)
-
-        cast(nc.vector.tensor_copy, 0, 0, 0, XC)
-        cast(scalar_cast, 0, 1, 0, XC)
-        cast(nc.vector.tensor_copy, 0, 2, 0, XC)
-        cast(nc.vector.tensor_copy, 0, 3, 0, V_COLS)
-        cast(scalar_cast, 0, 3, V_COLS, XC)
-        for i in range(T // XC):
-            cast(scalar_cast, 1, i, 0, XC)
+            src = raw[h][i][:, :, lo:hi].rearrange("p u c -> p c u")
+            if on_vector:
+                nc.vector.tensor_copy(out=dst, in_=src)
+            else:
+                nc.scalar.activation(dst, src, COPY)
 
         w_group = keep.tile([P, M, 4], BF16, name="w_group", align_bytes=64)
-        nc.gpsimd.tensor_scalar(
-            out=w_group[:], in0=w_raw[:].rearrange("p t m -> p m t"), scalar1=1.0, scalar2=0.0, op0=MULT, op1=ADD
-        )
         w_codes = keep.tile([P, M], U32, name="w_codes", align_bytes=64)
         w_scales = keep.tile([P, M], U8, name="w_scales", align_bytes=64)
+
+        def group_w(on_vector):
+            if on_vector:
+                nc.vector.tensor_copy(out=w_group[:], in_=w_raw[:].rearrange("p t m -> p m t"))
+            else:
+                nc.gpsimd.tensor_scalar(
+                    out=w_group[:], in0=w_raw[:].rearrange("p t m -> p m t"), scalar1=1.0, scalar2=0.0, op0=MULT, op1=ADD
+                )
+
+        def quantise_w():
+            nc.vector.quantize_mx(
+                out=w_codes[:].bitcast(FP8X4), scales=w_scales[:], in_=w_group[:].rearrange("p m t -> p (m t)")
+            )
 
         got = [[keep.tile([P, C], U32, name=f"got{h}_{q}") for q in range(Q)] for h in range(2)]
 
@@ -95,113 +96,184 @@ def tile_attend_grid_relu_kernel(tc, xT, w, part, bias, offs, out):
                 got[h][q][:], win[h][:].bitcast(U32).indirect(offsets[:, q * C // 16 : (q + 1) * C // 16])
             )
 
-        banks, terms, esum, turned, codes = {}, {}, {}, {}, {}
+        banks, terms, accs, turned, ys = {}, {}, {}, {}, {}
 
-        def forward(q):
-            ts = psum.tile([P, 2, 4, P], BF16, name="ts", tag="ts")
-            tv = psum.tile([P, 2, 4, P], BF16, name="tv", tag="tv")
-            banks[q] = (ts, tv)
-            for h in range(2):
-                src = got[h][q][:].bitcast(BF16).rearrange("p (g j u) -> p j u g", j=J, u=2)
-                for j in range(J):
-                    for u in range(2):
-                        nc.tensor.transpose((ts, tv)[j // 2][:, j % 2, 2 * h + u, :], src[:, j, u, :], ident_b[:])
+        def turn(h, q):
+            bank = psum4.tile([P, J, 2, P], BF16, name="bank")
+            src = got[h][q][:].bitcast(BF16).rearrange("p (g j u) -> p j u g", j=J, u=2)
+            for j in range(J):
+                for u in range(2):
+                    nc.tensor.transpose(bank[:, j, u, :], src[:, j, u, :], ident_b[:])
+            banks[h, q] = bank
 
-        def products(q):
-            p0 = ring.tile([P, 4, P], F32, name="p0")
-            p1 = ring.tile([P, 4, P], F32, name="p1")
-            terms[q] = (p0, p1)
-            for j, dst in ((0, p0), (1, p1)):
-                nc.scalar.activation(dst[:], banks[q][0][:, j, :, :], COPY, scale=part_t[:, j, q : q + 1])
+        def scalar_term(h, q, j):
+            p = ring3.tile([P, 2, P], F32, name=f"p{j}")
+            nc.scalar.activation(p[:], banks[h, q][:, j, :, :], COPY, scale=part_t[:, j, q : q + 1])
+            terms[h, q, j] = p
 
-        def sums(q):
-            a = ring.tile([P, 4, P], F32, name="a")
-            b = ring.tile([P, 4, P], F32, name="b")
-            e = ring.tile([P, 4, P], BF16, name="e")
-            for j, src, dst in ((2, terms[q][0], a), (3, terms[q][1], b)):
-                nc.vector.scalar_tensor_tensor(
-                    out=dst[:], in0=banks[q][1][:, j - 2, :, :], scalar=part_t[:, j, q : q + 1], in1=src[:], op0=MULT, op1=ADD
+        def vector_term(h, q, j, onto=None):
+            p = ring3.tile([P, 2, P], F32, name=f"p{j}")
+            if onto is None:
+                nc.vector.tensor_scalar(
+                    out=p[:], in0=banks[h, q][:, j, :, :], scalar1=part_t[:, j, q : q + 1], scalar2=None, op0=MULT
                 )
-            adder = nc.vector if q == Q - 1 else nc.gpsimd
-            adder.tensor_tensor(out=e[:], in0=a[:], in1=b[:], op=ADD)
-            esum[q] = e
+            else:
+                nc.vector.scalar_tensor_tensor(
+                    out=p[:], in0=banks[h, q][:, j, :, :], scalar=part_t[:, j, q : q + 1],
+                    in1=terms[h, q, onto][:], op0=MULT, op1=ADD,
+                )
+            terms[h, q, j] = p
 
-        def back(q):
-            tb = psum1.tile([P, 4, P], BF16, name="tb")
-            for t in range(4):
-                nc.tensor.transpose(tb[:, t, :], esum[q][:, t, :], ident_b[:])
+        def add_up(h, q, js):
+            for u in range(2):
+                for j in js:
+                    nc.tensor.matmul(
+                        accs[q][:, 2 * h + u, :], terms[h, q, j][:, u, :], ident_f[:],
+                        start=(j == js[0]), stop=(j == js[-1]), is_transpose=True,
+                    )
+
+        def open_sum(q):
+            accs[q] = psum.tile([P, 4, P], F32, name="acc", tag="acc")
+
+        def weigh(h, q, mode):
+            if mode == "S":
+                for j in range(4):
+                    scalar_term(h, q, j)
+                add_up(h, q, (0, 1, 2, 3))
+            elif mode == "SV":
+                scalar_term(h, q, 0)
+                scalar_term(h, q, 1)
+                vector_term(h, q, 2, 0)
+                vector_term(h, q, 3, 1)
+                add_up(h, q, (2, 3))
+            elif mode == "SSSV":
+                for j in (2, 0, 1):
+                    scalar_term(h, q, j)
+                vector_term(h, q, 3, 2)
+                add_up(h, q, (0, 1, 3))
+            elif mode == "SVVV":
+                scalar_term(h, q, 0)
+                for j in (1, 2, 3):
+                    vector_term(h, q, j, j - 1)
+                add_up(h, q, (3,))
+            elif mode == "S+V":
+                scalar_term(h, q, 0)
+                vector_term(h, q, 2)
+                scalar_term(h, q, 1)
+                vector_term(h, q, 3, 2)
+                add_up(h, q, (0, 1, 3))
+            else:
+                vector_term(h, q, 0)
+                vector_term(h, q, 1, 0)
+                vector_term(h, q, 2, 1)
+                vector_term(h, q, 3, 2)
+                add_up(h, q, (3,))
+
+        def group(q, on_vector):
             grouped = ring.tile([P, P, 4], BF16, name="grouped", align_bytes=64)
-            nc.scalar.copy(out=grouped[:], in_=tb[:].rearrange("p t g -> p g t"))
+            src = accs[q][:].rearrange("p t g -> p g t")
+            if on_vector:
+                nc.vector.tensor_copy(out=grouped[:], in_=src)
+            else:
+                nc.scalar.activation(grouped[:], src, COPY)
             turned[q] = grouped
 
+        e_codes = keep.tile([P, G], U32, name="e_codes", align_bytes=64)
+        e_scales = keep.tile([P, G], U8, name="e_scales", align_bytes=64)
+
         def quantise(q):
-            ec = ring.tile([P, P], U32, name="ec", align_bytes=64)
-            es = ring.tile([P, P], U8, name="es", align_bytes=64)
+            cols = slice(q * P, (q + 1) * P)
             nc.vector.quantize_mx(
-                out=ec[:].bitcast(FP8X4), scales=es[:], in_=turned[q][:].rearrange("p g t -> p (g t)")
+                out=e_codes[:, cols].bitcast(FP8X4), scales=e_scales[:, cols], in_=turned[q][:].rearrange("p g t -> p (g t)")
             )
-            codes[q] = (ec, es)
 
         out_rows = out.rearrange("(t p) g -> p t g", p=P)
 
-        def layer(q):
-            ec, es = codes[q]
-            o = ring.tile([P, MT, P], F32, name="o")
-            for half in range(2):
-                y = psum1.tile([P, 2, P], F32, name=f"y{half}")
-                for i in range(2):
-                    cols = slice((2 * half + i) * P, (2 * half + i + 1) * P)
-                    nc.tensor.matmul_mx(
-                        out=y[:, i, :],
-                        lhsT=w_codes[:, cols].bitcast(FP8X4),
-                        lhsT_scale=w_scales[:, cols],
-                        rhs=ec[:].bitcast(FP8X4),
-                        rhs_scale=es[:],
-                        start=True,
-                        stop=True,
-                    )
-                for i in range(2):
-                    mt = 2 * half + i
-                    if q == Q - 1 and half == 1:
-                        nc.vector.tensor_scalar(
-                            out=o[:, mt, :], in0=y[:, i, :], scalar1=bias_t[:, mt : mt + 1], scalar2=0.0, op0=ADD, op1=MAX
-                        )
-                    else:
-                        nc.scalar.activation(o[:, mt, :], y[:, i, :], RELU, bias=bias_t[:, mt : mt + 1])
-                nc.sync.dma_start(
-                    out=out_rows[:, 2 * half : 2 * half + 2, q * P : (q + 1) * P], in_=o[:, 2 * half : 2 * half + 2, :]
+        def multiply(q0, n, half):
+            y = psum1.tile([P, 2, n * P], F32, name=f"y{half}")
+            e_cols = slice(q0 * P, (q0 + n) * P)
+            for i in range(2):
+                cols = slice((2 * half + i) * P, (2 * half + i + 1) * P)
+                nc.tensor.matmul_mx(
+                    out=y[:, i, :],
+                    lhsT=w_codes[:, cols].bitcast(FP8X4),
+                    lhsT_scale=w_scales[:, cols],
+                    rhs=e_codes[:, e_cols].bitcast(FP8X4),
+                    rhs_scale=e_scales[:, e_cols],
+                    start=True,
+                    stop=True,
                 )
+            ys[q0, half] = y
 
-        for q in range(Q):
-            gather(0, q)
-        gather(1, 0)
-        forward(0)
-        products(0)
+        def finish(q0, n, half, on_vector):
+            o = ring.tile([P, 2, n * P], F32, name=f"o{half}")
+            y = ys[q0, half]
+            for i in range(2):
+                mt = 2 * half + i
+                if on_vector:
+                    nc.vector.tensor_scalar(
+                        out=o[:, i, :], in0=y[:, i, :], scalar1=bias_t[:, mt : mt + 1], scalar2=0.0, op0=ADD, op1=MAX
+                    )
+                else:
+                    nc.scalar.activation(o[:, i, :], y[:, i, :], RELU, bias=bias_t[:, mt : mt + 1])
+            nc.sync.dma_start(out=out_rows[:, 2 * half : 2 * half + 2, q0 * P : (q0 + n) * P], in_=o[:])
+
+        cast(0, 0, False)
+        parts()
+        cast(1, 0, False)
+        open_sum(0)
+        cast(0, 2, True)
+        cast(0, 1, True)
+        cast(1, 1, False)
+        cast(0, 3, True)
+        gather(0, 1)
+        gather(0, 2)
+        gather(0, 0)
+        group_w(False)
+        open_sum(1)
+        turn(0, 1)
+        turn(0, 0)
+        cast(1, 2, False)
+        cast(1, 3, True)
         gather(1, 1)
-        forward(1)
-        products(1)
-        sums(0)
-        gather(1, 2)
+        gather(1, 0)
+        gather(0, 3)
+        weigh(0, 1, "S")
+        turn(1, 1)
+        weigh(0, 0, "S")
+        turn(1, 0)
+        weigh(1, 1, "S")
+        turn(0, 2)
         gather(1, 3)
-        back(0)
-        forward(2)
-        products(2)
-        sums(1)
-        nc.vector.quantize_mx(
-            out=w_codes[:].bitcast(FP8X4), scales=w_scales[:], in_=w_group[:].rearrange("p m t -> p (m t)")
-        )
-        quantise(0)
-        layer(0)
-        back(1)
-        forward(3)
-        products(3)
-        sums(2)
+        gather(1, 2)
+        weigh(1, 0, "S")
+        group(1, False)
+        turn(1, 3)
+        turn(1, 2)
         quantise(1)
-        layer(1)
-        back(2)
-        sums(3)
+        group(0, True)
+        open_sum(3)
+        quantise_w()
+        turn(0, 3)
+        open_sum(2)
+        quantise(0)
+        multiply(0, 2, 0)
+        multiply(0, 2, 1)
+        weigh(0, 2, "SV")
+        weigh(1, 3, "SV")
+        weigh(1, 2, "SSSV")
+        finish(0, 2, 1, True)
+        group(2, True)
+        finish(0, 2, 0, False)
         quantise(2)
-        layer(2)
-        back(3)
+        weigh(0, 3, "S")
+        group(3, True)
+        multiply(2, 1, 1)
         quantise(3)
-        layer(3)
+        finish(2, 1, 1, False)
+        multiply(2, 1, 0)
+        finish(2, 1, 0, False)
+        multiply(3, 1, 1)
+        multiply(3, 1, 0)
+        finish(3, 1, 1, True)
+        finish(3, 1, 0, False)

@@ -29,12 +29,17 @@ def tile_attend_grid_relu_kernel(tc, xT, w, part, bias, offs, out):
         keep = ctx.enter_context(tc.tile_pool(name="keep", bufs=1))
         ring = ctx.enter_context(tc.tile_pool(name="ring", bufs=2))
         ring3 = ctx.enter_context(tc.tile_pool(name="ring3", bufs=3))
+        ring4 = ctx.enter_context(tc.tile_pool(name="ring4", bufs=4))
         psum4 = ctx.enter_context(tc.psum_pool(name="psum4", bufs=4))
         psum = ctx.enter_context(tc.psum_pool(name="psum", bufs=2))
         psum1 = ctx.enter_context(tc.psum_pool(name="psum1", bufs=1))
 
         rows = keep.tile([P, C], F32, name="rows")
-        nc.gpsimd.memset(rows[:], 0.0)
+        brow = keep.tile([P, P], F32, name="brow")
+        nc.vector.memset(rows[:], 0.0)
+        nc.vector.memset(brow[:], 0.0)
+        nc.scalar.dma_start(out=rows[0:Q, :], in_=part[0:1, :].rearrange("o (q c) -> (o q) c", q=Q))
+        nc.scalar.dma_start(out=brow[0:MT, :], in_=bias.rearrange("(t p) o -> t (p o)", p=P))
         offsets = keep.tile([P, G * J // 16], U16, name="offsets")
         nc.sync.dma_start(offsets[:], offs)
         x_rows = xT.rearrange("(p h u) c -> p h u c", h=2, u=2)
@@ -42,25 +47,24 @@ def tile_attend_grid_relu_kernel(tc, xT, w, part, bias, offs, out):
         for h in range(2):
             for i in range(T // XC):
                 nc.sync.dma_start(out=raw[h][i][:], in_=x_rows[:, h, :, i * XC : (i + 1) * XC])
-                if h == 0 and i == 1:
-                    nc.sync.dma_start(out=rows[0:Q, :], in_=part[0:1, :].rearrange("o (q c) -> (o q) c", q=Q))
         w_raw = keep.tile([P, 4, M], F32, name="w_raw")
         nc.sync.dma_start(out=w_raw[:], in_=w.rearrange("(p t) m -> p t m", t=4))
-        bias_t = keep.tile([P, MT], F32, name="bias_t")
-        nc.sync.dma_start(out=bias_t[:], in_=bias.rearrange("(t p) o -> p (t o)", p=P))
 
         ident_f = keep.tile([P, P], F32, name="ident_f")
         make_identity(nc, ident_f[:])
-        ident_b = keep.tile([P, P], BF16, name="ident_b")
-        make_identity(nc, ident_b[:])
 
         part_t = keep.tile([P, J, Q], F32, name="part_t")
 
+        bias_t = keep.tile([P, MT], F32, name="bias_t")
+
         def parts():
-            pt = psum.tile([P, J, P], F32, name="pt", tag="acc")
+            pt = psum4.tile([P, J, P], F32, name="pt", tag="bank")
             for j in range(J):
                 nc.tensor.transpose(pt[:, j, :], rows[:].rearrange("p (g j) -> p j g", j=J)[:, j, :], ident_f[:])
             nc.vector.tensor_copy(out=part_t[:], in_=pt[:, :, 0:Q])
+            bt = psum4.tile([P, P], F32, name="bt", tag="bank")
+            nc.tensor.transpose(bt[:], brow[:], ident_f[:])
+            nc.vector.tensor_copy(out=bias_t[:], in_=bt[:, 0:MT])
 
         win = [keep.tile([P, 2 * T], BF16, name=f"win{h}") for h in range(2)]
 
@@ -89,93 +93,87 @@ def tile_attend_grid_relu_kernel(tc, xT, w, part, bias, offs, out):
                 out=w_codes[:].bitcast(FP8X4), scales=w_scales[:], in_=w_group[:].rearrange("p m t -> p (m t)")
             )
 
-        got = [[keep.tile([P, C], U32, name=f"got{h}_{q}") for q in range(Q)] for h in range(2)]
+        got = [[keep.tile([P, J, P], U32, name=f"got{h}_{q}") for q in range(Q)] for h in range(2)]
 
         def gather(h, q):
             nc.vector.tensor_copy(
-                got[h][q][:], win[h][:].bitcast(U32).indirect(offsets[:, q * C // 16 : (q + 1) * C // 16])
+                got[h][q][:].rearrange("p j g -> p g j"),
+                win[h][:].bitcast(U32).indirect(offsets[:, q * C // 16 : (q + 1) * C // 16]),
             )
 
-        banks, terms, accs, turned, ys = {}, {}, {}, {}, {}
+        banks, terms, sums, backs, turned, ys = {}, {}, {}, {}, {}, {}
 
         def turn(h, q):
-            bank = psum4.tile([P, J, 2, P], BF16, name="bank")
-            src = got[h][q][:].bitcast(BF16).rearrange("p (g j u) -> p j u g", j=J, u=2)
+            bank = psum4.tile([P, J, P], F32, name="bank", tag="bank")
             for j in range(J):
-                for u in range(2):
-                    nc.tensor.transpose(bank[:, j, u, :], src[:, j, u, :], ident_b[:])
+                nc.tensor.transpose(bank[:, j, :], got[h][q][:, j, :].bitcast(F32), ident_f[:])
             banks[h, q] = bank
 
+        def corner(h, q, j):
+            return banks[h, q][:, j, :].bitcast(BF16)
+
         def scalar_term(h, q, j):
-            p = ring3.tile([P, 2, P], F32, name=f"p{j}")
-            nc.scalar.activation(p[:], banks[h, q][:, j, :, :], COPY, scale=part_t[:, j, q : q + 1])
+            p = ring3.tile([P, 2 * P], F32, name=f"p{j}")
+            nc.scalar.activation(p[:], corner(h, q, j), COPY, scale=part_t[:, j, q : q + 1])
             terms[h, q, j] = p
 
-        def vector_term(h, q, j, onto=None):
-            p = ring3.tile([P, 2, P], F32, name=f"p{j}")
+        def new_sum(h, q):
+            sums[h, q] = ring4.tile([P, 2 * P], BF16, name="e")
+            return sums[h, q]
+
+        def vector_term(h, q, j, onto=None, last=False):
+            p = new_sum(h, q) if last else ring3.tile([P, 2 * P], F32, name=f"p{j}")
             if onto is None:
                 nc.vector.tensor_scalar(
-                    out=p[:], in0=banks[h, q][:, j, :, :], scalar1=part_t[:, j, q : q + 1], scalar2=None, op0=MULT
+                    out=p[:], in0=corner(h, q, j), scalar1=part_t[:, j, q : q + 1], scalar2=None, op0=MULT
                 )
             else:
                 nc.vector.scalar_tensor_tensor(
-                    out=p[:], in0=banks[h, q][:, j, :, :], scalar=part_t[:, j, q : q + 1],
-                    in1=terms[h, q, onto][:], op0=MULT, op1=ADD,
+                    out=p[:], in0=corner(h, q, j), scalar=part_t[:, j, q : q + 1], in1=terms[h, q, onto][:], op0=MULT, op1=ADD
                 )
             terms[h, q, j] = p
 
-        def add_up(h, q, js):
-            for u in range(2):
-                for j in js:
-                    nc.tensor.matmul(
-                        accs[q][:, 2 * h + u, :], terms[h, q, j][:, u, :], ident_f[:],
-                        start=(j == js[0]), stop=(j == js[-1]), is_transpose=True,
-                    )
-
-        def open_sum(q):
-            accs[q] = psum.tile([P, 4, P], F32, name="acc", tag="acc")
+        def add(engine, h, q, a, b):
+            engine.tensor_tensor(out=new_sum(h, q)[:], in0=terms[h, q, a][:], in1=terms[h, q, b][:], op=ADD)
 
         def weigh(h, q, mode):
-            if mode == "S":
-                for j in range(4):
-                    scalar_term(h, q, j)
-                add_up(h, q, (0, 1, 2, 3))
-            elif mode == "SV":
+            if mode in ("SVG", "SVV"):
                 scalar_term(h, q, 0)
                 scalar_term(h, q, 1)
                 vector_term(h, q, 2, 0)
                 vector_term(h, q, 3, 1)
-                add_up(h, q, (2, 3))
-            elif mode == "SSSV":
-                for j in (2, 0, 1):
+                add(nc.gpsimd if mode == "SVG" else nc.vector, h, q, 2, 3)
+            elif mode == "SSSVG":
+                for j in (0, 1, 2):
                     scalar_term(h, q, j)
                 vector_term(h, q, 3, 2)
-                add_up(h, q, (0, 1, 3))
-            elif mode == "SVVV":
-                scalar_term(h, q, 0)
-                for j in (1, 2, 3):
-                    vector_term(h, q, j, j - 1)
-                add_up(h, q, (3,))
-            elif mode == "S+V":
-                scalar_term(h, q, 0)
-                vector_term(h, q, 2)
-                scalar_term(h, q, 1)
-                vector_term(h, q, 3, 2)
-                add_up(h, q, (0, 1, 3))
+                g = ring3.tile([P, 2 * P], F32, name="g")
+                nc.gpsimd.tensor_tensor(out=g[:], in0=terms[h, q, 0][:], in1=terms[h, q, 1][:], op=ADD)
+                terms[h, q, 0] = g
+                add(nc.gpsimd, h, q, 0, 3)
             else:
-                vector_term(h, q, 0)
+                if mode == "SVVV":
+                    scalar_term(h, q, 0)
+                else:
+                    vector_term(h, q, 0)
                 vector_term(h, q, 1, 0)
                 vector_term(h, q, 2, 1)
-                vector_term(h, q, 3, 2)
-                add_up(h, q, (3,))
+                vector_term(h, q, 3, 2, last=True)
+
+        def back(q):
+            tb = psum.tile([P, 2, P], F32, name="tb")
+            for h in range(2):
+                nc.tensor.transpose(tb[:, h, :], sums[h, q][:].bitcast(F32), ident_f[:])
+            backs[q] = tb
 
         def group(q, on_vector):
             grouped = ring.tile([P, P, 4], BF16, name="grouped", align_bytes=64)
-            src = accs[q][:].rearrange("p t g -> p g t")
+            dst = grouped[:].rearrange("p g t -> p (g t)").bitcast(F32).rearrange("p (g h) -> p g h", h=2)
+            src = backs[q][:].rearrange("p h g -> p g h")
             if on_vector:
-                nc.vector.tensor_copy(out=grouped[:], in_=src)
+                nc.vector.tensor_copy(out=dst, in_=src)
             else:
-                nc.scalar.activation(grouped[:], src, COPY)
+                nc.scalar.copy(out=dst, in_=src)
             turned[q] = grouped
 
         e_codes = keep.tile([P, G], U32, name="e_codes", align_bytes=64)
@@ -219,61 +217,61 @@ def tile_attend_grid_relu_kernel(tc, xT, w, part, bias, offs, out):
             nc.sync.dma_start(out=out_rows[:, 2 * half : 2 * half + 2, q0 * P : (q0 + n) * P], in_=o[:])
 
         cast(0, 0, False)
-        parts()
-        cast(1, 0, False)
-        open_sum(0)
-        cast(0, 2, True)
         cast(0, 1, True)
-        cast(1, 1, False)
+        parts()
+        cast(0, 2, True)
+        group_w(False)
+        cast(1, 0, False)
         cast(0, 3, True)
         gather(0, 1)
-        gather(0, 2)
+        cast(1, 1, False)
         gather(0, 0)
-        group_w(False)
-        open_sum(1)
-        turn(0, 1)
-        turn(0, 0)
         cast(1, 2, False)
-        cast(1, 3, True)
+        cast(1, 3, False)
+        gather(0, 2)
+        gather(0, 3)
+        turn(0, 0)
+        turn(0, 1)
         gather(1, 1)
         gather(1, 0)
-        gather(0, 3)
-        weigh(0, 1, "S")
         turn(1, 1)
-        weigh(0, 0, "S")
-        turn(1, 0)
-        weigh(1, 1, "S")
-        turn(0, 2)
-        gather(1, 3)
+        weigh(0, 0, "SVG")
         gather(1, 2)
-        weigh(1, 0, "S")
-        group(1, False)
-        turn(1, 3)
-        turn(1, 2)
-        quantise(1)
-        group(0, True)
-        open_sum(3)
+        weigh(0, 1, "SSSVG")
         quantise_w()
+        weigh(1, 1, "SSSVG")
+        turn(1, 0)
+        turn(1, 2)
+        turn(0, 2)
+        weigh(1, 0, "SVV")
+        back(0)
+        back(1)
+        gather(1, 3)
+        weigh(0, 2, "SSSVG")
+        group(0, False)
+        group(1, True)
         turn(0, 3)
-        open_sum(2)
         quantise(0)
-        multiply(0, 2, 0)
+        quantise(1)
+        weigh(1, 2, "SVG")
+        turn(1, 3)
+        weigh(0, 3, "SVG")
+        weigh(1, 3, "SVV")
         multiply(0, 2, 1)
-        weigh(0, 2, "SV")
-        weigh(1, 3, "SV")
-        weigh(1, 2, "SSSV")
-        finish(0, 2, 1, True)
-        group(2, True)
+        multiply(0, 2, 0)
+        finish(0, 2, 1, False)
         finish(0, 2, 0, False)
+        back(2)
+        back(3)
+        group(2, True)
         quantise(2)
-        weigh(0, 3, "S")
-        group(3, True)
         multiply(2, 1, 1)
-        quantise(3)
         finish(2, 1, 1, False)
         multiply(2, 1, 0)
-        finish(2, 1, 0, False)
+        group(3, True)
+        quantise(3)
+        finish(2, 1, 0, True)
         multiply(3, 1, 1)
-        multiply(3, 1, 0)
         finish(3, 1, 1, True)
+        multiply(3, 1, 0)
         finish(3, 1, 0, False)

@@ -28,8 +28,8 @@ def tile_attend_grid_relu_kernel(tc, xT, w, part, bias, offs, out):
     with ExitStack() as ctx:
         keep = ctx.enter_context(tc.tile_pool(name="keep", bufs=1))
         ring = ctx.enter_context(tc.tile_pool(name="ring", bufs=2))
-        ring3 = ctx.enter_context(tc.tile_pool(name="ring3", bufs=3))
-        ring4 = ctx.enter_context(tc.tile_pool(name="ring4", bufs=4))
+        ring3 = ctx.enter_context(tc.tile_pool(name="ring3", bufs=6))
+        ring4 = ctx.enter_context(tc.tile_pool(name="ring4", bufs=8))
         psum4 = ctx.enter_context(tc.psum_pool(name="psum4", bufs=4))
         psum = ctx.enter_context(tc.psum_pool(name="psum", bufs=2))
         psum1 = ctx.enter_context(tc.psum_pool(name="psum1", bufs=1))
@@ -101,7 +101,7 @@ def tile_attend_grid_relu_kernel(tc, xT, w, part, bias, offs, out):
                 win[h][:].bitcast(U32).indirect(offsets[:, q * C // 16 : (q + 1) * C // 16]),
             )
 
-        banks, terms, sums, backs, turned, ys = {}, {}, {}, {}, {}, {}
+        banks, terms, sums, backs, turned, ys, outs = {}, {}, {}, {}, {}, {}, {}
 
         def turn(h, q):
             bank = psum4.tile([P, J, P], F32, name="bank", tag="bank")
@@ -136,35 +136,15 @@ def tile_attend_grid_relu_kernel(tc, xT, w, part, bias, offs, out):
         def add(engine, h, q, a, b):
             engine.tensor_tensor(out=new_sum(h, q)[:], in0=terms[h, q, a][:], in1=terms[h, q, b][:], op=ADD)
 
-        def weigh(h, q, mode):
-            if mode in ("SVG", "SVV"):
-                scalar_term(h, q, 0)
-                scalar_term(h, q, 1)
-                vector_term(h, q, 2, 0)
-                vector_term(h, q, 3, 1)
-                add(nc.gpsimd if mode == "SVG" else nc.vector, h, q, 2, 3)
-            elif mode == "SSSVG":
-                for j in (0, 1, 2):
-                    scalar_term(h, q, j)
-                vector_term(h, q, 3, 2)
-                g = ring3.tile([P, 2 * P], F32, name="g")
-                nc.gpsimd.tensor_tensor(out=g[:], in0=terms[h, q, 0][:], in1=terms[h, q, 1][:], op=ADD)
-                terms[h, q, 0] = g
-                add(nc.gpsimd, h, q, 0, 3)
-            else:
-                if mode == "SVVV":
-                    scalar_term(h, q, 0)
-                else:
-                    vector_term(h, q, 0)
-                vector_term(h, q, 1, 0)
-                vector_term(h, q, 2, 1)
-                vector_term(h, q, 3, 2, last=True)
+        def add_terms(h, q, a, b):
+            g = ring3.tile([P, 2 * P], F32, name="g")
+            nc.gpsimd.tensor_tensor(out=g[:], in0=terms[h, q, a][:], in1=terms[h, q, b][:], op=ADD)
+            terms[h, q, a] = g
 
-        def back(q):
-            tb = psum.tile([P, 2, P], F32, name="tb")
-            for h in range(2):
-                nc.tensor.transpose(tb[:, h, :], sums[h, q][:].bitcast(F32), ident_f[:])
-            backs[q] = tb
+        def back(h, q):
+            if q not in backs:
+                backs[q] = psum.tile([P, 2, P], F32, name="tb")
+            nc.tensor.transpose(backs[q][:, h, :], sums[h, q][:].bitcast(F32), ident_f[:])
 
         def group(q, on_vector):
             grouped = ring.tile([P, P, 4], BF16, name="grouped", align_bytes=64)
@@ -203,75 +183,130 @@ def tile_attend_grid_relu_kernel(tc, xT, w, part, bias, offs, out):
                 )
             ys[q0, half] = y
 
-        def finish(q0, n, half, on_vector):
-            o = ring.tile([P, 2, n * P], F32, name=f"o{half}")
-            y = ys[q0, half]
-            for i in range(2):
-                mt = 2 * half + i
-                if on_vector:
-                    nc.vector.tensor_scalar(
-                        out=o[:, i, :], in0=y[:, i, :], scalar1=bias_t[:, mt : mt + 1], scalar2=0.0, op0=ADD, op1=MAX
-                    )
-                else:
-                    nc.scalar.activation(o[:, i, :], y[:, i, :], RELU, bias=bias_t[:, mt : mt + 1])
-            nc.sync.dma_start(out=out_rows[:, 2 * half : 2 * half + 2, q0 * P : (q0 + n) * P], in_=o[:])
+        def finish(q0, n, half, i, on_vector):
+            if (q0, half) not in outs:
+                outs[q0, half] = ring.tile([P, 2, n * P], F32, name=f"o{half}")
+            o, y, mt = outs[q0, half], ys[q0, half], 2 * half + i
+            if on_vector:
+                nc.vector.tensor_scalar(
+                    out=o[:, i, :], in0=y[:, i, :], scalar1=bias_t[:, mt : mt + 1], scalar2=0.0, op0=ADD, op1=MAX
+                )
+            else:
+                nc.scalar.activation(o[:, i, :], y[:, i, :], RELU, bias=bias_t[:, mt : mt + 1])
 
-        cast(0, 0, False)
+        def store(q0, n, half):
+            nc.sync.dma_start(
+                out=out_rows[:, 2 * half : 2 * half + 2, q0 * P : (q0 + n) * P], in_=outs[q0, half][:]
+            )
+
+        cast(0, 0, True)
         cast(0, 1, True)
-        parts()
         cast(0, 2, True)
-        group_w(False)
-        cast(1, 0, False)
         cast(0, 3, True)
+        gather(0, 0)
+        cast(1, 0, False)
         gather(0, 1)
         cast(1, 1, False)
-        gather(0, 0)
-        cast(1, 2, False)
-        cast(1, 3, False)
-        gather(0, 2)
-        gather(0, 3)
         turn(0, 0)
+        parts()
+        gather(0, 3)
         turn(0, 1)
+        cast(1, 2, False)
+        cast(1, 3, True)
+        scalar_term(0, 1, 0)
+        turn(0, 3)
+        scalar_term(0, 1, 1)
+        scalar_term(0, 1, 2)
+        gather(1, 3)
+        add_terms(0, 1, 0, 1)
+        scalar_term(0, 3, 0)
+        scalar_term(0, 3, 1)
+        scalar_term(0, 0, 0)
         gather(1, 1)
+        scalar_term(0, 0, 3)
+        turn(1, 3)
+        group_w(False)
+        scalar_term(0, 0, 2)
+        scalar_term(0, 0, 1)
+        scalar_term(1, 3, 0)
         gather(1, 0)
         turn(1, 1)
-        weigh(0, 0, "SVG")
+        scalar_term(1, 3, 1)
+        scalar_term(1, 3, 2)
         gather(1, 2)
-        weigh(0, 1, "SSSVG")
+        scalar_term(1, 1, 0)
+        add_terms(1, 3, 0, 1)
+        add_terms(0, 0, 2, 3)
         quantise_w()
-        weigh(1, 1, "SSSVG")
-        turn(1, 0)
+        add_terms(0, 0, 0, 1)
+        vector_term(1, 3, 3, 2)
+        vector_term(0, 3, 3, 1)
         turn(1, 2)
+        vector_term(0, 3, 2, 0)
+        add(nc.gpsimd, 1, 3, 0, 3)
+        vector_term(0, 1, 3, 2)
+        turn(1, 0)
+        vector_term(1, 1, 1, 0)
+        add(nc.gpsimd, 0, 3, 2, 3)
+        scalar_term(1, 2, 0)
+        gather(0, 2)
+        scalar_term(1, 2, 3)
+        add(nc.gpsimd, 0, 1, 0, 3)
+        scalar_term(1, 0, 0)
+        back(0, 3)
+        back(1, 3)
+        scalar_term(1, 0, 1)
+        vector_term(1, 1, 2, 1)
+        add(nc.gpsimd, 0, 0, 0, 2)
         turn(0, 2)
-        weigh(1, 0, "SVV")
-        back(0)
-        back(1)
-        gather(1, 3)
-        weigh(0, 2, "SSSVG")
-        group(0, False)
-        group(1, True)
-        turn(0, 3)
-        quantise(0)
-        quantise(1)
-        weigh(1, 2, "SVG")
-        turn(1, 3)
-        weigh(0, 3, "SVG")
-        weigh(1, 3, "SVV")
-        multiply(0, 2, 1)
-        multiply(0, 2, 0)
-        finish(0, 2, 1, False)
-        finish(0, 2, 0, False)
-        back(2)
-        back(3)
-        group(2, True)
-        quantise(2)
-        multiply(2, 1, 1)
-        finish(2, 1, 1, False)
-        multiply(2, 1, 0)
-        group(3, True)
+        group(3, False)
+        vector_term(1, 0, 3, 1)
+        scalar_term(1, 2, 2)
+        vector_term(1, 0, 2, 0)
+        back(0, 1)
+        scalar_term(1, 2, 1)
+        back(0, 0)
+        vector_term(1, 1, 3, 2, last=True)
+        add_terms(1, 2, 2, 3)
+        scalar_term(0, 2, 0)
+        add(nc.vector, 1, 0, 2, 3)
+        back(1, 1)
         quantise(3)
-        finish(2, 1, 0, True)
+        back(1, 0)
+        vector_term(0, 2, 1, 0)
         multiply(3, 1, 1)
-        finish(3, 1, 1, True)
+        add_terms(1, 2, 0, 1)
+        group(1, True)
         multiply(3, 1, 0)
-        finish(3, 1, 0, False)
+        group(0, False)
+        vector_term(0, 2, 2, 1)
+        finish(3, 1, 1, 0, False)
+        quantise(1)
+        add(nc.gpsimd, 1, 2, 0, 2)
+        finish(3, 1, 1, 1, False)
+        store(3, 1, 1)
+        quantise(0)
+        finish(3, 1, 0, 0, True)
+        finish(3, 1, 0, 1, True)
+        store(3, 1, 0)
+        multiply(0, 2, 1)
+        vector_term(0, 2, 3, 2, last=True)
+        multiply(0, 2, 0)
+        back(0, 2)
+        back(1, 2)
+        finish(0, 2, 1, 0, False)
+        finish(0, 2, 1, 1, False)
+        store(0, 2, 1)
+        group(2, True)
+        finish(0, 2, 0, 0, False)
+        quantise(2)
+        finish(0, 2, 0, 1, False)
+        store(0, 2, 0)
+        multiply(2, 1, 1)
+        multiply(2, 1, 0)
+        finish(2, 1, 1, 0, True)
+        finish(2, 1, 1, 1, True)
+        store(2, 1, 1)
+        finish(2, 1, 0, 0, False)
+        finish(2, 1, 0, 1, False)
+        store(2, 1, 0)

from contextlib import ExitStack

import concourse.mybir as mybir
from concourse.masks import make_identity

G, J, T, D, M = 512, 4, 2048, 512, 512
P = 128
FLOPS = 2 * D * M * G
BYTES = 4 * (D * T + D * M + G * J + M + M * G) + 2 * P * G * J // 16

F32 = mybir.dt.float32
BF16 = mybir.dt.bfloat16
U32 = mybir.dt.uint32
U16 = mybir.dt.uint16
U8 = mybir.dt.uint8
FP8X4 = mybir.dt.float8_e4m3fn_x4
ADD, MULT, MAX = mybir.AluOpType.add, mybir.AluOpType.mult, mybir.AluOpType.max
COPY, RELU = mybir.ActivationFunctionType.Copy, mybir.ActivationFunctionType.Relu

Q = G // P
C = P * J
MT = M // P
XC = 512


def tile_attend_grid_relu_kernel(tc, xT, w, part, bias, offs, out):
    nc = tc.nc
    with ExitStack() as ctx:
        keep = ctx.enter_context(tc.tile_pool(name="keep", bufs=1))
        ring = ctx.enter_context(tc.tile_pool(name="ring", bufs=2))
        ring3 = ctx.enter_context(tc.tile_pool(name="ring3", bufs=6))
        ring4 = ctx.enter_context(tc.tile_pool(name="ring4", bufs=8))
        psum4 = ctx.enter_context(tc.psum_pool(name="psum4", bufs=4))
        psum = ctx.enter_context(tc.psum_pool(name="psum", bufs=2))
        psum1 = ctx.enter_context(tc.psum_pool(name="psum1", bufs=1))

        rows = keep.tile([P, C], F32, name="rows")
        brow = keep.tile([P, P], F32, name="brow")
        nc.vector.memset(rows[:], 0.0)
        nc.vector.memset(brow[:], 0.0)
        nc.scalar.dma_start(out=rows[0:Q, :], in_=part[0:1, :].rearrange("o (q c) -> (o q) c", q=Q))
        nc.scalar.dma_start(out=brow[0:MT, :], in_=bias.rearrange("(t p) o -> t (p o)", p=P))
        offsets = keep.tile([P, G * J // 16], U16, name="offsets")
        nc.sync.dma_start(offsets[:], offs)
        x_rows = xT.rearrange("(p h u) c -> p h u c", h=2, u=2)
        raw = [[keep.tile([P, 2, XC], F32, name=f"raw{h}_{i}") for i in range(T // XC)] for h in range(2)]
        for h in range(2):
            for i in range(T // XC):
                nc.sync.dma_start(out=raw[h][i][:], in_=x_rows[:, h, :, i * XC : (i + 1) * XC])
        w_raw = keep.tile([P, 4, M], F32, name="w_raw")
        nc.sync.dma_start(out=w_raw[:], in_=w.rearrange("(p t) m -> p t m", t=4))

        ident_f = keep.tile([P, P], F32, name="ident_f")
        make_identity(nc, ident_f[:])

        part_t = keep.tile([P, J, Q], F32, name="part_t")

        bias_t = keep.tile([P, MT], F32, name="bias_t")

        def parts():
            pt = psum4.tile([P, J, P], F32, name="pt", tag="bank")
            for j in range(J):
                nc.tensor.transpose(pt[:, j, :], rows[:].rearrange("p (g j) -> p j g", j=J)[:, j, :], ident_f[:])
            nc.vector.tensor_copy(out=part_t[:], in_=pt[:, :, 0:Q])
            bt = psum4.tile([P, P], F32, name="bt", tag="bank")
            nc.tensor.transpose(bt[:], brow[:], ident_f[:])
            nc.vector.tensor_copy(out=bias_t[:], in_=bt[:, 0:MT])

        win = [keep.tile([P, 2 * T], BF16, name=f"win{h}") for h in range(2)]

        def cast(h, i, on_vector, lo=0, hi=XC):
            dst = win[h][:, 2 * (i * XC + lo) : 2 * (i * XC + hi)].rearrange("p (c u) -> p c u", u=2)
            src = raw[h][i][:, :, lo:hi].rearrange("p u c -> p c u")
            if on_vector:
                nc.vector.tensor_copy(out=dst, in_=src)
            else:
                nc.scalar.activation(dst, src, COPY)

        w_group = keep.tile([P, M, 4], BF16, name="w_group", align_bytes=64)
        w_codes = keep.tile([P, M], U32, name="w_codes", align_bytes=64)
        w_scales = keep.tile([P, M], U8, name="w_scales", align_bytes=64)

        def group_w(on_vector):
            if on_vector:
                nc.vector.tensor_copy(out=w_group[:], in_=w_raw[:].rearrange("p t m -> p m t"))
            else:
                nc.gpsimd.tensor_scalar(
                    out=w_group[:], in0=w_raw[:].rearrange("p t m -> p m t"), scalar1=1.0, scalar2=0.0, op0=MULT, op1=ADD
                )

        def quantise_w():
            nc.vector.quantize_mx(
                out=w_codes[:].bitcast(FP8X4), scales=w_scales[:], in_=w_group[:].rearrange("p m t -> p (m t)")
            )

        got = [[keep.tile([P, J, P], U32, name=f"got{h}_{q}") for q in range(Q)] for h in range(2)]

        def gather(h, q):
            nc.vector.tensor_copy(
                got[h][q][:].rearrange("p j g -> p g j"),
                win[h][:].bitcast(U32).indirect(offsets[:, q * C // 16 : (q + 1) * C // 16]),
            )

        banks, terms, sums, backs, turned, ys, outs = {}, {}, {}, {}, {}, {}, {}

        def turn(h, q):
            bank = psum4.tile([P, J, P], F32, name="bank", tag="bank")
            for j in range(J):
                nc.tensor.transpose(bank[:, j, :], got[h][q][:, j, :].bitcast(F32), ident_f[:])
            banks[h, q] = bank

        def corner(h, q, j):
            return banks[h, q][:, j, :].bitcast(BF16)

        def scalar_term(h, q, j):
            p = ring3.tile([P, 2 * P], F32, name=f"p{j}")
            nc.scalar.activation(p[:], corner(h, q, j), COPY, scale=part_t[:, j, q : q + 1])
            terms[h, q, j] = p

        def new_sum(h, q):
            sums[h, q] = ring4.tile([P, 2 * P], BF16, name="e")
            return sums[h, q]

        def vector_term(h, q, j, onto=None, last=False):
            p = new_sum(h, q) if last else ring3.tile([P, 2 * P], F32, name=f"p{j}")
            if onto is None:
                nc.vector.tensor_scalar(
                    out=p[:], in0=corner(h, q, j), scalar1=part_t[:, j, q : q + 1], scalar2=None, op0=MULT
                )
            else:
                nc.vector.scalar_tensor_tensor(
                    out=p[:], in0=corner(h, q, j), scalar=part_t[:, j, q : q + 1], in1=terms[h, q, onto][:], op0=MULT, op1=ADD
                )
            terms[h, q, j] = p

        def add(engine, h, q, a, b):
            engine.tensor_tensor(out=new_sum(h, q)[:], in0=terms[h, q, a][:], in1=terms[h, q, b][:], op=ADD)

        def add_terms(h, q, a, b):
            g = ring3.tile([P, 2 * P], F32, name="g")
            nc.gpsimd.tensor_tensor(out=g[:], in0=terms[h, q, a][:], in1=terms[h, q, b][:], op=ADD)
            terms[h, q, a] = g

        def back(h, q):
            if q not in backs:
                backs[q] = psum.tile([P, 2, P], F32, name="tb")
            nc.tensor.transpose(backs[q][:, h, :], sums[h, q][:].bitcast(F32), ident_f[:])

        def group(q, on_vector):
            grouped = ring.tile([P, P, 4], BF16, name="grouped", align_bytes=64)
            dst = grouped[:].rearrange("p g t -> p (g t)").bitcast(F32).rearrange("p (g h) -> p g h", h=2)
            src = backs[q][:].rearrange("p h g -> p g h")
            if on_vector:
                nc.vector.tensor_copy(out=dst, in_=src)
            else:
                nc.scalar.copy(out=dst, in_=src)
            turned[q] = grouped

        e_codes = keep.tile([P, G], U32, name="e_codes", align_bytes=64)
        e_scales = keep.tile([P, G], U8, name="e_scales", align_bytes=64)

        def quantise(q):
            cols = slice(q * P, (q + 1) * P)
            nc.vector.quantize_mx(
                out=e_codes[:, cols].bitcast(FP8X4), scales=e_scales[:, cols], in_=turned[q][:].rearrange("p g t -> p (g t)")
            )

        out_rows = out.rearrange("(t p) g -> p t g", p=P)

        def multiply(q0, n, half):
            y = psum1.tile([P, 2, n * P], F32, name=f"y{half}")
            e_cols = slice(q0 * P, (q0 + n) * P)
            for i in range(2):
                cols = slice((2 * half + i) * P, (2 * half + i + 1) * P)
                nc.tensor.matmul_mx(
                    out=y[:, i, :],
                    lhsT=w_codes[:, cols].bitcast(FP8X4),
                    lhsT_scale=w_scales[:, cols],
                    rhs=e_codes[:, e_cols].bitcast(FP8X4),
                    rhs_scale=e_scales[:, e_cols],
                    start=True,
                    stop=True,
                )
            ys[q0, half] = y

        def finish(q0, n, half, i, on_vector):
            if (q0, half) not in outs:
                outs[q0, half] = ring.tile([P, 2, n * P], F32, name=f"o{half}")
            o, y, mt = outs[q0, half], ys[q0, half], 2 * half + i
            if on_vector:
                nc.vector.tensor_scalar(
                    out=o[:, i, :], in0=y[:, i, :], scalar1=bias_t[:, mt : mt + 1], scalar2=0.0, op0=ADD, op1=MAX
                )
            else:
                nc.scalar.activation(o[:, i, :], y[:, i, :], RELU, bias=bias_t[:, mt : mt + 1])

        def store(q0, n, half):
            nc.sync.dma_start(
                out=out_rows[:, 2 * half : 2 * half + 2, q0 * P : (q0 + n) * P], in_=outs[q0, half][:]
            )

        cast(0, 0, True)
        cast(0, 1, True)
        cast(0, 2, True)
        cast(0, 3, True)
        gather(0, 0)
        cast(1, 0, False)
        gather(0, 1)
        cast(1, 1, False)
        turn(0, 0)
        parts()
        gather(0, 3)
        turn(0, 1)
        cast(1, 2, False)
        cast(1, 3, True)
        scalar_term(0, 1, 0)
        turn(0, 3)
        scalar_term(0, 1, 1)
        scalar_term(0, 1, 2)
        gather(1, 3)
        add_terms(0, 1, 0, 1)
        scalar_term(0, 3, 0)
        scalar_term(0, 3, 1)
        scalar_term(0, 0, 0)
        gather(1, 1)
        scalar_term(0, 0, 3)
        turn(1, 3)
        group_w(False)
        scalar_term(0, 0, 2)
        scalar_term(0, 0, 1)
        scalar_term(1, 3, 0)
        gather(1, 0)
        turn(1, 1)
        scalar_term(1, 3, 1)
        scalar_term(1, 3, 2)
        gather(1, 2)
        scalar_term(1, 1, 0)
        add_terms(1, 3, 0, 1)
        add_terms(0, 0, 2, 3)
        quantise_w()
        add_terms(0, 0, 0, 1)
        vector_term(1, 3, 3, 2)
        vector_term(0, 3, 3, 1)
        turn(1, 2)
        vector_term(0, 3, 2, 0)
        add(nc.gpsimd, 1, 3, 0, 3)
        vector_term(0, 1, 3, 2)
        turn(1, 0)
        vector_term(1, 1, 1, 0)
        add(nc.gpsimd, 0, 3, 2, 3)
        scalar_term(1, 2, 0)
        gather(0, 2)
        scalar_term(1, 2, 3)
        add(nc.gpsimd, 0, 1, 0, 3)
        scalar_term(1, 0, 0)
        back(0, 3)
        back(1, 3)
        scalar_term(1, 0, 1)
        vector_term(1, 1, 2, 1)
        add(nc.gpsimd, 0, 0, 0, 2)
        turn(0, 2)
        group(3, False)
        vector_term(1, 0, 3, 1)
        scalar_term(1, 2, 2)
        vector_term(1, 0, 2, 0)
        back(0, 1)
        scalar_term(1, 2, 1)
        back(0, 0)
        vector_term(1, 1, 3, 2, last=True)
        add_terms(1, 2, 2, 3)
        scalar_term(0, 2, 0)
        add(nc.vector, 1, 0, 2, 3)
        back(1, 1)
        quantise(3)
        back(1, 0)
        vector_term(0, 2, 1, 0)
        multiply(3, 1, 1)
        add_terms(1, 2, 0, 1)
        group(1, True)
        multiply(3, 1, 0)
        group(0, False)
        vector_term(0, 2, 2, 1)
        finish(3, 1, 1, 0, False)
        quantise(1)
        add(nc.gpsimd, 1, 2, 0, 2)
        finish(3, 1, 1, 1, False)
        store(3, 1, 1)
        quantise(0)
        finish(3, 1, 0, 0, True)
        finish(3, 1, 0, 1, True)
        store(3, 1, 0)
        multiply(0, 2, 1)
        vector_term(0, 2, 3, 2, last=True)
        multiply(0, 2, 0)
        back(0, 2)
        back(1, 2)
        finish(0, 2, 1, 0, False)
        finish(0, 2, 1, 1, False)
        store(0, 2, 1)
        group(2, True)
        finish(0, 2, 0, 0, False)
        quantise(2)
        finish(0, 2, 0, 1, False)
        store(0, 2, 0)
        multiply(2, 1, 1)
        multiply(2, 1, 0)
        finish(2, 1, 1, 0, True)
        finish(2, 1, 1, 1, True)
        store(2, 1, 1)
        finish(2, 1, 0, 0, False)
        finish(2, 1, 0, 1, False)
        store(2, 1, 0)
